import numpy as np
import ml_dtypes


def mxq(x, axis, fmt="e4m3"):
    dtype, down = {"e4m3": (ml_dtypes.float8_e4m3fn, 7), "e5m2": (ml_dtypes.float8_e5m2, 14)}[fmt]
    v = np.moveaxis(np.asarray(x, np.float32).astype(ml_dtypes.bfloat16).astype(np.float64), axis, -1)
    blocks = v.reshape(v.shape[:-1] + (-1, 32))
    amax = np.abs(blocks).max(-1, keepdims=True)
    byte = np.maximum(np.where(amax > 0, np.frexp(amax)[1] - 1 + 127, 0) - down, 1)
    scale = np.exp2(byte - 127.0)
    codes = (blocks / scale).astype(np.float32).astype(dtype).astype(np.float64)
    return np.moveaxis((codes * scale).reshape(v.shape), -1, axis)


WIDE = False


def mx_kscale(k):
    if not WIDE:
        return np.ones(k)
    levels = np.array([10, -10, 5, -5, 0])
    if k % 512:
        return np.exp2(np.random.permutation(np.resize(levels, k // 32))).repeat(32)
    a = np.empty((k // 512, 16))
    for p in range(k // 512):
        a[p, :8] = np.random.permutation(np.resize(levels, 8))
        for g in range(8):
            far = levels[np.abs(levels - a[p, g]) >= 10]
            a[p, g + 8] = far[np.random.randint(len(far))]
    return np.exp2(a.ravel()).repeat(32)


def f64(x):
    return np.asarray(x).astype(np.float64)


def striped(idx):
    return np.tile(idx.reshape(-1, 16).T, (8, 1)).astype(np.uint16)


def unstriped(offs):
    return offs[:16].T.reshape(-1).astype(np.int64)


def pack_weight(w):
    k, n = w.shape
    w = f64(np.asarray(w, np.float32).astype(ml_dtypes.bfloat16)).reshape(k // 32, 32, n)
    amax = np.abs(w).max(1)
    byte = np.clip(np.where(amax > 0, np.frexp(amax)[1] - 1 + 127 - 7, 1), 1, 254)
    scaled = (w * np.exp2(127.0 - byte)[:, None, :]).reshape(k, n).astype(np.float32)
    words = np.ascontiguousarray(scaled.reshape(k // 512, 128, 4, n).transpose(0, 1, 3, 2)).astype(ml_dtypes.float8_e4m3fn).view(np.uint8)
    return words, np.ascontiguousarray(byte.astype(np.uint8).reshape(k // 512, 16, n))


def unpack_weight(words, scales):
    g, p, n, _ = words.shape
    vals = np.ascontiguousarray(words).view(ml_dtypes.float8_e4m3fn).astype(np.float64) * np.repeat(np.exp2(scales.astype(np.float64) - 127.0), 8, axis=1)[..., None]
    return vals.transpose(0, 1, 3, 2).reshape(g * 512, n)


K, T, S, V = 1024, 1024, 512, 512
P = 2 ** 7


def setup_inputs():
    n = np.random.standard_normal
    s = mx_kscale(K)[:, None]
    packed_xT = pack_weight(n((K, T)) * s)
    return {
        "x_words": packed_xT[0],
        "x_scales": packed_xT[1],
        "hT": (n((K, V)) / np.sqrt(K) / s).astype(np.float32),
        "cooc": (np.random.uniform(0.0, 1.0, (V, S)) ** 3 * 30 + 0.5).astype(np.float32),
        "cap": (np.tile(np.random.uniform(0.8, 1.0, S), (P, 1))).astype(np.float32),
        "ctxb": (np.tile(0.5 * n(T), (P, 1))).astype(np.float32),
        "tgtb": (0.5 * n((V, 1))).astype(np.float32),
        "offs": striped(np.random.permutation(T)[:S]),
    }


def reference(x_words, x_scales, hT, cooc, cap, ctxb, tgtb, offs):
    lx = np.log(f64(cooc))
    wt = np.minimum(np.exp(0.75 * (lx - 2.3)), f64(cap)[:1])
    hTq = mxq(f64(hT), 0, "e4m3")
    xq = unpack_weight(x_words, x_scales)[:, unstriped(offs)]
    y = hTq.T @ xq
    err = y + f64(ctxb)[:1][:, unstriped(offs)] - lx + f64(tgtb)
    return wt * ((err) ** 2)

@@ -1,0 +1,162 @@
+from contextlib import ExitStack
+
+import concourse.mybir as mybir
+from concourse.masks import make_identity
+
+K, T, S, V = 1024, 1024, 512, 512
+FLOPS = 2 * K * V * S
+
+F32 = mybir.dt.float32
+BF16 = mybir.dt.bfloat16
+I32 = mybir.dt.int32
+U32 = mybir.dt.uint32
+U16 = mybir.dt.uint16
+U8 = mybir.dt.uint8
+FP8X4 = mybir.dt.float8_e4m3fn_x4
+ALU = mybir.AluOpType
+ACT = mybir.ActivationFunctionType
+
+P = 128
+PACK = 4
+PASSES = K // (P * PACK)
+TILES = V // P
+POWER = 0.75
+SHIFT = 2.3
+
+
+def tile_picked_yglovw_loss_p_kernel(
+    tc, x_words, x_scales, hT, cooc, cap, ctxb, tgtb, offs, out
+):
+    nc = tc.nc
+    with ExitStack() as ctx:
+        keep = ctx.enter_context(tc.tile_pool(name="keep", bufs=1))
+        psum = ctx.enter_context(tc.psum_pool(name="psum", bufs=1))
+
+        offsets = keep.tile([P, S // 16], U16, name="offsets")
+        nc.sync.dma_start(offsets[:], offs)
+
+        scale_table = keep.tile([P, T], U8, name="scale_table", align_bytes=64)
+        nc.gpsimd.memset(scale_table[:].bitcast(I32), 0)
+        ctx_row = keep.tile([P, T], F32, name="ctx_row")
+        nc.sync.dma_start(ctx_row[0:32, :], ctxb[0:32, :])
+        warm = keep.tile([P, 2], F32, name="warm")
+        nc.vector.memset(warm[:, 0:1], 1.0)
+        nc.vector.memset(ctx_row[32:64, :], 0.0)
+        nc.vector.memset(ctx_row[64:128, :], 0.0)
+        small_rows = keep.tile([P, P], F32, name="small_rows")
+        nc.vector.memset(small_rows[:], 0.0)
+        ident = keep.tile([P, P], F32, name="ident")
+        make_identity(nc, ident[:])
+
+        counts = [keep.tile([P, 2, S], F32, name=f"counts{a}") for a in range(2)]
+        cooc_v = cooc.rearrange("(a b p) j -> a p b j", a=2, b=2)
+        for a in range(2):
+            nc.sync.dma_start(counts[a][:], cooc_v[a])
+
+        scales_i32 = x_scales.bitcast(I32)
+        for q in range(4):
+            nc.sync.dma_start(
+                scale_table[32 * q : 32 * q + 8, :].bitcast(I32), scales_i32[:, 4 * q : 4 * q + 4, :]
+            )
+        nc.scalar.activation(warm[:, 1:2], warm[:, 0:1], ACT.Ln)
+
+        word_table = [keep.tile([P, T], I32, name=f"word_table{g}") for g in range(PASSES)]
+        for g in range(PASSES):
+            nc.sync.dma_start(word_table[g][:], x_words[g].rearrange("p c r -> p (c r)").bitcast(I32))
+
+        nc.sync.dma_start(small_rows[0:4, :], cap[0:1, :].rearrange("o (c p) -> (o c) p", p=P))
+        nc.sync.dma_start(small_rows[4:8, :], tgtb.rearrange("(c p) o -> c (p o)", p=P))
+
+        pieces = [(0, 256, 0, "v"), (0, 256, 1, "v"), (256, 256, 0, "s"), (256, 128, 1, "s"), (384, 128, 1, "s")]
+        h_v = hT.rearrange("(g p j) t -> g p j t", g=PASSES, j=PACK)
+        raw = []
+        for i, (c0, w, g, eng) in enumerate(pieces):
+            r = keep.tile([P, PACK, w], F32, name=f"raw{i}")
+            nc.sync.dma_start(r[:], h_v[g][:, :, c0 : c0 + w])
+            raw.append(r)
+
+        ctx_picked = keep.tile([P, S], F32, name="ctx_picked")
+        nc.vector.tensor_copy(ctx_picked[:], ctx_row[:].indirect(offsets[:]))
+        x_scale = keep.tile([P, S], U8, name="x_scale", align_bytes=64)
+        nc.vector.tensor_copy(x_scale[:], scale_table[:].indirect(offsets[:]))
+
+        ctx_turned = psum.tile([P, TILES, P], F32, name="ctx_turned")
+        for c in range(TILES):
+            nc.tensor.transpose(ctx_turned[:, c, :], ctx_picked[:, c * P : (c + 1) * P], ident[:])
+        ctx_cols = keep.tile([P, TILES], F32, name="ctx_cols")
+        nc.vector.tensor_copy(ctx_cols[:], ctx_turned[:, :, 0])
+        ctx_wide = psum.tile([P, S], F32, name="ctx_wide")
+        for c in range(TILES):
+            nc.tensor.transpose(
+                ctx_wide[:, c * P : (c + 1) * P], ctx_cols[:, c : c + 1].to_broadcast([P, P]), ident[:]
+            )
+        ctx_all = keep.tile([P, S], F32, name="ctx_all")
+        nc.vector.tensor_copy(ctx_all[:], ctx_wide[:])
+
+        logc = keep.tile([P, 2, 2, S], F32, name="logc")
+        for a in range(2):
+            nc.scalar.activation(logc[:, a], counts[a][:], ACT.Ln)
+
+        x_code = [keep.tile([P, S], U32, name=f"x_code{g}", align_bytes=64) for g in range(PASSES)]
+        nc.vector.tensor_copy(x_code[0][:], word_table[0][:].bitcast(U32).indirect(offsets[:]))
+
+        small_turned = psum.tile([P, P], F32, name="small_turned")
+        nc.tensor.transpose(small_turned[:], small_rows[:], ident[:])
+        small_cols = keep.tile([P, 8], F32, name="small_cols")
+        nc.vector.tensor_copy(small_cols[:], small_turned[:, 0:8])
+        cap_wide = psum.tile([P, S], F32, name="cap_wide")
+        for c in range(TILES):
+            nc.tensor.transpose(
+                cap_wide[:, c * P : (c + 1) * P], small_cols[:, c : c + 1].to_broadcast([P, P]), ident[:]
+            )
+
+        diff = [keep.tile([P, S], F32, name=f"diff{m}") for m in range(TILES)]
+        nc.vector.tensor_copy(x_code[1][:], word_table[1][:].bitcast(U32).indirect(offsets[:]))
+        for m in range(TILES):
+            nc.gpsimd.tensor_tensor(diff[m][:], ctx_all[:], logc[:, m // 2, m % 2, :], ALU.subtract)
+
+        powered = keep.tile([P, 2, 2, S], F32, name="powered")
+        for b in range(2):
+            nc.scalar.activation(powered[:, :, b, :], logc[:, :, b, :], ACT.Exp, bias=-POWER * SHIFT, scale=POWER)
+        weight = [keep.tile([P, S], F32, name=f"weight{m}") for m in range(TILES)]
+        for m in (0, 2, 1, 3):
+            nc.vector.tensor_tensor(weight[m][:], powered[:, m // 2, m % 2, :], cap_wide[:], ALU.min)
+
+        acc = [psum.tile([P, S], F32, name=f"acc{m}") for m in range(TILES)]
+        for i, (c0, w, g, eng) in enumerate(pieces):
+            woven = keep.tile([P, w * PACK], BF16, name=f"woven{i}", align_bytes=64)
+            dst = woven[:].rearrange("p (c i j) -> p c j i", i=4, j=PACK)
+            src = raw[i][:].rearrange("p j (c i) -> p c j i", i=4)
+            if eng == "v":
+                nc.vector.tensor_copy(dst, src)
+            else:
+                nc.scalar.copy(dst, src)
+            h_code = keep.tile([P, w], U32, name=f"h_code{i}", align_bytes=64)
+            h_scale = keep.tile([P, w], U8, name=f"h_scale{i}", align_bytes=64)
+            nc.vector.quantize_mx(out=h_code[:].bitcast(FP8X4), scales=h_scale[:], in_=woven[:])
+            for c in range(0, w, P):
+                m = (c0 + c) // P
+                nc.tensor.matmul_mx(
+                    out=acc[m][:],
+                    lhsT=h_code[:, c : c + P].bitcast(FP8X4),
+                    lhsT_scale=h_scale[:, c : c + P],
+                    rhs=x_code[g][:].bitcast(FP8X4),
+                    rhs_scale=x_scale[4 * g : P, :],
+                    start=(g == 0),
+                    stop=(g == PASSES - 1),
+                )
+            if g == PASSES - 1:
+                for c in range(0, w, P):
+                    m = (c0 + c) // P
+                    err = keep.tile([P, S], F32, name=f"err{m}")
+                    nc.vector.scalar_tensor_tensor(
+                        err[:], acc[m][:], small_cols[:, 4 + m : 5 + m], diff[m][:], ALU.add, ALU.add
+                    )
+                    sq = keep.tile([P, S], F32, name=f"sq{m}")
+                    nc.scalar.activation(sq[:], err[:], ACT.Square)
+                    res = keep.tile([P, S], F32, name=f"res{m}")
+                    if m < 2:
+                        nc.gpsimd.tensor_tensor(res[:], sq[:], weight[m][:], ALU.mult)
+                    else:
+                        nc.vector.tensor_tensor(res[:], sq[:], weight[m][:], ALU.mult)
+                    nc.sync.dma_start(out[m * P : (m + 1) * P, :], res[:])

@@ -36,13 +36,9 @@ def tile_picked_yglovw_loss_p_kernel(
         nc.sync.dma_start(offsets[:], offs)
 
         scale_table = keep.tile([P, T], U8, name="scale_table", align_bytes=64)
-        nc.gpsimd.memset(scale_table[:].bitcast(I32), 0)
-        ctx_row = keep.tile([P, T], F32, name="ctx_row")
-        nc.sync.dma_start(ctx_row[0:32, :], ctxb[0:32, :])
+        nc.vector.memset(scale_table[:].bitcast(I32), 0)
         warm = keep.tile([P, 2], F32, name="warm")
-        nc.vector.memset(warm[:, 0:1], 1.0)
-        nc.vector.memset(ctx_row[32:64, :], 0.0)
-        nc.vector.memset(ctx_row[64:128, :], 0.0)
+        nc.gpsimd.memset(warm[:, 0:1], 1.0)
         small_rows = keep.tile([P, P], F32, name="small_rows")
         nc.vector.memset(small_rows[:], 0.0)
         ident = keep.tile([P, P], F32, name="ident")
@@ -50,24 +46,24 @@ def tile_picked_yglovw_loss_p_kernel(
 
         counts = [keep.tile([P, 2, S], F32, name=f"counts{a}") for a in range(2)]
         cooc_v = cooc.rearrange("(a b p) j -> a p b j", a=2, b=2)
-        for a in range(2):
-            nc.sync.dma_start(counts[a][:], cooc_v[a])
-
+        nc.sync.dma_start(counts[0][:], cooc_v[0])
         scales_i32 = x_scales.bitcast(I32)
         for q in range(4):
             nc.sync.dma_start(
                 scale_table[32 * q : 32 * q + 8, :].bitcast(I32), scales_i32[:, 4 * q : 4 * q + 4, :]
             )
+        nc.sync.dma_start(counts[1][:], cooc_v[1])
+        ctx_table = keep.tile([P, T], F32, name="ctx_table")
+        nc.sync.dma_start(ctx_table[:], ctxb)
+        nc.sync.dma_start(small_rows[0:4, :], cap[0:1, :].rearrange("o (c p) -> (o c) p", p=P))
+        nc.sync.dma_start(small_rows[4:8, :], tgtb.rearrange("(c p) o -> c (p o)", p=P))
         nc.scalar.activation(warm[:, 1:2], warm[:, 0:1], ACT.Ln)
 
         word_table = [keep.tile([P, T], I32, name=f"word_table{g}") for g in range(PASSES)]
         for g in range(PASSES):
             nc.sync.dma_start(word_table[g][:], x_words[g].rearrange("p c r -> p (c r)").bitcast(I32))
 
-        nc.sync.dma_start(small_rows[0:4, :], cap[0:1, :].rearrange("o (c p) -> (o c) p", p=P))
-        nc.sync.dma_start(small_rows[4:8, :], tgtb.rearrange("(c p) o -> c (p o)", p=P))
-
-        pieces = [(0, 256, 0, "v"), (0, 256, 1, "v"), (256, 256, 0, "s"), (256, 128, 1, "s"), (384, 128, 1, "s")]
+        pieces = [(0, 256, 0, "v"), (0, 256, 1, "s"), (256, 256, 0, "s"), (256, 128, 1, "s"), (384, 128, 1, "s")]
         h_v = hT.rearrange("(g p j) t -> g p j t", g=PASSES, j=PACK)
         raw = []
         for i, (c0, w, g, eng) in enumerate(pieces):
@@ -75,30 +71,10 @@ def tile_picked_yglovw_loss_p_kernel(
             nc.sync.dma_start(r[:], h_v[g][:, :, c0 : c0 + w])
             raw.append(r)
 
-        ctx_picked = keep.tile([P, S], F32, name="ctx_picked")
-        nc.vector.tensor_copy(ctx_picked[:], ctx_row[:].indirect(offsets[:]))
         x_scale = keep.tile([P, S], U8, name="x_scale", align_bytes=64)
         nc.vector.tensor_copy(x_scale[:], scale_table[:].indirect(offsets[:]))
-
-        ctx_turned = psum.tile([P, TILES, P], F32, name="ctx_turned")
-        for c in range(TILES):
-            nc.tensor.transpose(ctx_turned[:, c, :], ctx_picked[:, c * P : (c + 1) * P], ident[:])
-        ctx_cols = keep.tile([P, TILES], F32, name="ctx_cols")
-        nc.vector.tensor_copy(ctx_cols[:], ctx_turned[:, :, 0])
-        ctx_wide = psum.tile([P, S], F32, name="ctx_wide")
-        for c in range(TILES):
-            nc.tensor.transpose(
-                ctx_wide[:, c * P : (c + 1) * P], ctx_cols[:, c : c + 1].to_broadcast([P, P]), ident[:]
-            )
-        ctx_all = keep.tile([P, S], F32, name="ctx_all")
-        nc.vector.tensor_copy(ctx_all[:], ctx_wide[:])
-
-        logc = keep.tile([P, 2, 2, S], F32, name="logc")
-        for a in range(2):
-            nc.scalar.activation(logc[:, a], counts[a][:], ACT.Ln)
-
-        x_code = [keep.tile([P, S], U32, name=f"x_code{g}", align_bytes=64) for g in range(PASSES)]
-        nc.vector.tensor_copy(x_code[0][:], word_table[0][:].bitcast(U32).indirect(offsets[:]))
+        ctx_picked = keep.tile([P, S], F32, name="ctx_picked")
+        nc.vector.tensor_copy(ctx_picked[:], ctx_table[:].indirect(offsets[:]))
 
         small_turned = psum.tile([P, P], F32, name="small_turned")
         nc.tensor.transpose(small_turned[:], small_rows[:], ident[:])
@@ -110,22 +86,47 @@ def tile_picked_yglovw_loss_p_kernel(
                 cap_wide[:, c * P : (c + 1) * P], small_cols[:, c : c + 1].to_broadcast([P, P]), ident[:]
             )
 
+        logc = keep.tile([P, 2, 2, S], F32, name="logc")
+        for a in range(2):
+            nc.scalar.activation(logc[:, a], counts[a][:], ACT.Ln)
+
+        x_code = [keep.tile([P, S], U32, name=f"x_code{g}", align_bytes=64) for g in range(PASSES)]
+        for g in range(PASSES):
+            nc.vector.tensor_copy(x_code[g][:], word_table[g][:].bitcast(U32).indirect(offsets[:]))
+
         diff = [keep.tile([P, S], F32, name=f"diff{m}") for m in range(TILES)]
-        nc.vector.tensor_copy(x_code[1][:], word_table[1][:].bitcast(U32).indirect(offsets[:]))
         for m in range(TILES):
-            nc.gpsimd.tensor_tensor(diff[m][:], ctx_all[:], logc[:, m // 2, m % 2, :], ALU.subtract)
+            nc.gpsimd.tensor_tensor(diff[m][:], ctx_picked[:], logc[:, m // 2, m % 2, :], ALU.subtract)
 
         powered = keep.tile([P, 2, 2, S], F32, name="powered")
         for b in range(2):
             nc.scalar.activation(powered[:, :, b, :], logc[:, :, b, :], ACT.Exp, bias=-POWER * SHIFT, scale=POWER)
-        weight = [keep.tile([P, S], F32, name=f"weight{m}") for m in range(TILES)]
-        for m in (0, 2, 1, 3):
-            nc.vector.tensor_tensor(weight[m][:], powered[:, m // 2, m % 2, :], cap_wide[:], ALU.min)
+        flat = [r[:].rearrange("p j t -> p (j t)") for r in raw]
+        weight = [flat[b].rearrange("p (a s) -> p a s", a=2) for b in range(2)]
 
-        acc = [psum.tile([P, S], F32, name=f"acc{m}") for m in range(TILES)]
-        for i, (c0, w, g, eng) in enumerate(pieces):
-            woven = keep.tile([P, w * PACK], BF16, name=f"woven{i}", align_bytes=64)
-            dst = woven[:].rearrange("p (c i j) -> p c j i", i=4, j=PACK)
+        def cap_weights(b):
+            nc.vector.tensor_tensor(
+                weight[b], powered[:, :, b, :], cap_wide[:].unsqueeze(1).to_broadcast([P, 2, S]), ALU.min
+            )
+
+        H = S // 2
+        spans = [[(0, S)]] * (TILES - 1) + [[(0, H), (H, S)]]
+        acc = [
+            [psum.tile([P, b - a], F32, name=f"acc{m}_{a}") for a, b in spans[m]] for m in range(TILES)
+        ]
+        sq = [flat[4], flat[3], flat[2][:, 0:S], flat[2][:, S : 2 * S]]
+        err = [keep.tile([P, S], F32, name=f"err{m}", align_bytes=64) for m in range(TILES)]
+        res = [keep.tile([P, S], F32, name=f"res{m}") for m in range(TILES)]
+        res[2] = diff[3]
+
+        def product(i):
+            c0, w, g, eng = pieces[i]
+            if i == 4:
+                woven = err[2][:, 0 : w * PACK // 2].bitcast(BF16)
+            else:
+                woven_tile = keep.tile([P, w * PACK], BF16, name=f"woven{i}", align_bytes=64)
+                woven = woven_tile[:]
+            dst = woven.rearrange("p (c i j) -> p c j i", i=4, j=PACK)
             src = raw[i][:].rearrange("p j (c i) -> p c j i", i=4)
             if eng == "v":
                 nc.vector.tensor_copy(dst, src)
@@ -133,30 +134,46 @@ def tile_picked_yglovw_loss_p_kernel(
                 nc.scalar.copy(dst, src)
             h_code = keep.tile([P, w], U32, name=f"h_code{i}", align_bytes=64)
             h_scale = keep.tile([P, w], U8, name=f"h_scale{i}", align_bytes=64)
-            nc.vector.quantize_mx(out=h_code[:].bitcast(FP8X4), scales=h_scale[:], in_=woven[:])
+            nc.vector.quantize_mx(out=h_code[:].bitcast(FP8X4), scales=h_scale[:], in_=woven)
             for c in range(0, w, P):
                 m = (c0 + c) // P
-                nc.tensor.matmul_mx(
-                    out=acc[m][:],
-                    lhsT=h_code[:, c : c + P].bitcast(FP8X4),
-                    lhsT_scale=h_scale[:, c : c + P],
-                    rhs=x_code[g][:].bitcast(FP8X4),
-                    rhs_scale=x_scale[4 * g : P, :],
-                    start=(g == 0),
-                    stop=(g == PASSES - 1),
-                )
-            if g == PASSES - 1:
-                for c in range(0, w, P):
-                    m = (c0 + c) // P
-                    err = keep.tile([P, S], F32, name=f"err{m}")
-                    nc.vector.scalar_tensor_tensor(
-                        err[:], acc[m][:], small_cols[:, 4 + m : 5 + m], diff[m][:], ALU.add, ALU.add
+                for n, (a, b) in enumerate(spans[m]):
+                    nc.tensor.matmul_mx(
+                        out=acc[m][n][:],
+                        lhsT=h_code[:, c : c + P].bitcast(FP8X4),
+                        lhsT_scale=h_scale[:, c : c + P],
+                        rhs=x_code[g][:, a:b].bitcast(FP8X4),
+                        rhs_scale=x_scale[4 * g : P, a:b],
+                        start=(g == 0),
+                        stop=(g == PASSES - 1),
                     )
-                    sq = keep.tile([P, S], F32, name=f"sq{m}")
-                    nc.scalar.activation(sq[:], err[:], ACT.Square)
-                    res = keep.tile([P, S], F32, name=f"res{m}")
-                    if m < 2:
-                        nc.gpsimd.tensor_tensor(res[:], sq[:], weight[m][:], ALU.mult)
-                    else:
-                        nc.vector.tensor_tensor(res[:], sq[:], weight[m][:], ALU.mult)
-                    nc.sync.dma_start(out[m * P : (m + 1) * P, :], res[:])
+
+        def error(m, n=0):
+            a, b = spans[m][n]
+            nc.vector.scalar_tensor_tensor(
+                err[m][:, a:b], acc[m][n][:], small_cols[:, 4 + m : 5 + m], diff[m][:, a:b], ALU.add, ALU.add
+            )
+
+        def finish(m, engine, n=0):
+            a, b = spans[m][n]
+            nc.scalar.activation(sq[m][:, a:b], err[m][:, a:b], ACT.Square)
+            engine.tensor_tensor(res[m][:, a:b], sq[m][:, a:b], weight[m % 2][:, m // 2, a:b], ALU.mult)
+            nc.sync.dma_start(out[m * P : (m + 1) * P, a:b], res[m][:, a:b])
+
+        product(0)
+        cap_weights(0)
+        product(1)
+        cap_weights(1)
+        error(0)
+        product(2)
+        error(1)
+        product(3)
+        product(4)
+        finish(0, nc.gpsimd)
+        error(2)
+        finish(1, nc.gpsimd)
+        error(3, 0)
+        error(3, 1)
+        finish(2, nc.vector)
+        finish(3, nc.vector, 0)
+        finish(3, nc.vector, 1)

@@ -52,9 +52,9 @@ def tile_picked_yglovw_loss_p_kernel(
             nc.sync.dma_start(
                 scale_table[32 * q : 32 * q + 8, :].bitcast(I32), scales_i32[:, 4 * q : 4 * q + 4, :]
             )
-        nc.sync.dma_start(counts[1][:], cooc_v[1])
         ctx_table = keep.tile([P, T], F32, name="ctx_table")
         nc.sync.dma_start(ctx_table[:], ctxb)
+        nc.sync.dma_start(counts[1][:], cooc_v[1])
         nc.sync.dma_start(small_rows[0:4, :], cap[0:1, :].rearrange("o (c p) -> (o c) p", p=P))
         nc.sync.dma_start(small_rows[4:8, :], tgtb.rearrange("(c p) o -> c (p o)", p=P))
         nc.scalar.activation(warm[:, 1:2], warm[:, 0:1], ACT.Ln)
@@ -90,13 +90,18 @@ def tile_picked_yglovw_loss_p_kernel(
         for a in range(2):
             nc.scalar.activation(logc[:, a], counts[a][:], ACT.Ln)
 
+        diff = [keep.tile([P, S], F32, name=f"diff{m}", align_bytes=64) for m in range(TILES)]
+
+        def difference(m, engine):
+            engine.tensor_tensor(diff[m][:], ctx_picked[:], logc[:, m // 2, m % 2, :], ALU.subtract)
+
+        difference(0, nc.vector)
+        difference(1, nc.vector)
+
         x_code = [keep.tile([P, S], U32, name=f"x_code{g}", align_bytes=64) for g in range(PASSES)]
         for g in range(PASSES):
             nc.vector.tensor_copy(x_code[g][:], word_table[g][:].bitcast(U32).indirect(offsets[:]))
 
-        diff = [keep.tile([P, S], F32, name=f"diff{m}") for m in range(TILES)]
-        for m in range(TILES):
-            nc.gpsimd.tensor_tensor(diff[m][:], ctx_picked[:], logc[:, m // 2, m % 2, :], ALU.subtract)
 
         powered = keep.tile([P, 2, 2, S], F32, name="powered")
         for b in range(2):
@@ -115,14 +120,18 @@ def tile_picked_yglovw_loss_p_kernel(
             [psum.tile([P, b - a], F32, name=f"acc{m}_{a}") for a, b in spans[m]] for m in range(TILES)
         ]
         sq = [flat[4], flat[3], flat[2][:, 0:S], flat[2][:, S : 2 * S]]
-        err = [keep.tile([P, S], F32, name=f"err{m}", align_bytes=64) for m in range(TILES)]
-        res = [keep.tile([P, S], F32, name=f"res{m}") for m in range(TILES)]
-        res[2] = diff[3]
+        pair = keep.tile([P, 2 * S], F32, name="pair", align_bytes=64)
+        err_tiles = [keep.tile([P, S], F32, name=f"err{m}") for m in (0, 1, 3)]
+        err = [err_tiles[0][:], err_tiles[1][:], pair[:, 0:S], err_tiles[2][:]]
+        res_tiles = [keep.tile([P, S], F32, name=f"res{m}") for m in (1, 3)]
+        res = [pair[:, S : 2 * S], res_tiles[0][:], diff[3][:], res_tiles[1][:]]
 
         def product(i):
             c0, w, g, eng = pieces[i]
             if i == 4:
-                woven = err[2][:, 0 : w * PACK // 2].bitcast(BF16)
+                woven = pair[:, S - P : S + P].bitcast(BF16)
+            elif i < 2:
+                woven = diff[2 + i][:].bitcast(BF16)
             else:
                 woven_tile = keep.tile([P, w * PACK], BF16, name=f"woven{i}", align_bytes=64)
                 woven = woven_tile[:]
@@ -162,18 +171,20 @@ def tile_picked_yglovw_loss_p_kernel(
 
         product(0)
         cap_weights(0)
+        difference(2, nc.gpsimd)
         product(1)
         cap_weights(1)
-        error(0)
+        difference(3, nc.gpsimd)
         product(2)
-        error(1)
+        error(0)
         product(3)
         product(4)
+        error(1)
         finish(0, nc.gpsimd)
         error(2)
-        finish(1, nc.gpsimd)
         error(3, 0)
         error(3, 1)
+        finish(1, nc.vector)
         finish(2, nc.vector)
         finish(3, nc.vector, 0)
         finish(3, nc.vector, 1)

@@ -20,56 +20,61 @@ P = 128
 PACK = 4
 PASSES = K // (P * PACK)
 TILES = V // P
+QUADRANTS = P // 32
+SCALE_ROWS = 4
+RUN = 4
 POWER = 0.75
 SHIFT = 2.3
+
+PIECES = [(0, 2 * P, 0), (0, 2 * P, 1), (2 * P, 2 * P, 0), (2 * P, P, 1), (3 * P, P, 1)]
+FIRST, LAST = 0, len(PIECES) - 1
+SPANS = [[(0, S)]] * (TILES - 1) + [[(0, S // 2), (S // 2, S)]]
 
 
 def tile_picked_yglovw_loss_p_kernel(
     tc, x_words, x_scales, hT, cooc, cap, ctxb, tgtb, offs, out
 ):
     nc = tc.nc
-    with ExitStack() as ctx:
-        keep = ctx.enter_context(tc.tile_pool(name="keep", bufs=1))
-        psum = ctx.enter_context(tc.psum_pool(name="psum", bufs=1))
+    with ExitStack() as stack:
+        keep = stack.enter_context(tc.tile_pool(name="keep", bufs=1))
+        psum = stack.enter_context(tc.psum_pool(name="psum", bufs=1))
 
         offsets = keep.tile([P, S // 16], U16, name="offsets")
         nc.sync.dma_start(offsets[:], offs)
 
         scale_table = keep.tile([P, T], U8, name="scale_table", align_bytes=64)
         nc.vector.memset(scale_table[:].bitcast(I32), 0)
-        warm = keep.tile([P, 2], F32, name="warm")
-        nc.gpsimd.memset(warm[:, 0:1], 1.0)
         small_rows = keep.tile([P, P], F32, name="small_rows")
         nc.vector.memset(small_rows[:], 0.0)
         ident = keep.tile([P, P], F32, name="ident")
         make_identity(nc, ident[:])
 
         counts = [keep.tile([P, 2, S], F32, name=f"counts{a}") for a in range(2)]
-        cooc_v = cooc.rearrange("(a b p) j -> a p b j", a=2, b=2)
-        nc.sync.dma_start(counts[0][:], cooc_v[0])
+        cooc_tiles = cooc.rearrange("(a b p) j -> a p b j", a=2, b=2)
+        nc.sync.dma_start(counts[0][:], cooc_tiles[0])
         scales_i32 = x_scales.bitcast(I32)
-        for q in range(4):
+        for q in range(QUADRANTS):
             nc.sync.dma_start(
-                scale_table[32 * q : 32 * q + 8, :].bitcast(I32), scales_i32[:, 4 * q : 4 * q + 4, :]
+                scale_table[32 * q : 32 * q + PASSES * SCALE_ROWS, :].bitcast(I32),
+                scales_i32[:, SCALE_ROWS * q : SCALE_ROWS * (q + 1), :],
             )
         ctx_table = keep.tile([P, T], F32, name="ctx_table")
         nc.sync.dma_start(ctx_table[:], ctxb)
-        nc.sync.dma_start(counts[1][:], cooc_v[1])
-        nc.sync.dma_start(small_rows[0:4, :], cap[0:1, :].rearrange("o (c p) -> (o c) p", p=P))
-        nc.sync.dma_start(small_rows[4:8, :], tgtb.rearrange("(c p) o -> c (p o)", p=P))
-        nc.scalar.activation(warm[:, 1:2], warm[:, 0:1], ACT.Ln)
+        nc.sync.dma_start(counts[1][:], cooc_tiles[1])
 
         word_table = [keep.tile([P, T], I32, name=f"word_table{g}") for g in range(PASSES)]
-        for g in range(PASSES):
-            nc.sync.dma_start(word_table[g][:], x_words[g].rearrange("p c r -> p (c r)").bitcast(I32))
+        words_i32 = [x_words[g].rearrange("p c r -> p (c r)").bitcast(I32) for g in range(PASSES)]
+        nc.sync.dma_start(word_table[0][:], words_i32[0])
+        nc.sync.dma_start(small_rows[0:TILES, :], cap[0:1, :].rearrange("o (c p) -> (o c) p", p=P))
+        nc.sync.dma_start(small_rows[TILES : 2 * TILES, :], tgtb.rearrange("(c p) o -> c (p o)", p=P))
+        nc.sync.dma_start(word_table[1][:], words_i32[1])
 
-        pieces = [(0, 256, 0, "v"), (0, 256, 1, "s"), (256, 256, 0, "s"), (256, 128, 1, "s"), (384, 128, 1, "s")]
-        h_v = hT.rearrange("(g p j) t -> g p j t", g=PASSES, j=PACK)
+        h_passes = hT.rearrange("(g p j) t -> g p j t", g=PASSES, j=PACK)
         raw = []
-        for i, (c0, w, g, eng) in enumerate(pieces):
-            r = keep.tile([P, PACK, w], F32, name=f"raw{i}")
-            nc.sync.dma_start(r[:], h_v[g][:, :, c0 : c0 + w])
-            raw.append(r)
+        for i, (first, width, g) in enumerate(PIECES):
+            piece = keep.tile([P, PACK, width], F32, name=f"raw{i}")
+            nc.sync.dma_start(piece[:], h_passes[g][:, :, first : first + width])
+            raw.append(piece)
 
         x_scale = keep.tile([P, S], U8, name="x_scale", align_bytes=64)
         nc.vector.tensor_copy(x_scale[:], scale_table[:].indirect(offsets[:]))
@@ -78,8 +83,8 @@ def tile_picked_yglovw_loss_p_kernel(
 
         small_turned = psum.tile([P, P], F32, name="small_turned")
         nc.tensor.transpose(small_turned[:], small_rows[:], ident[:])
-        small_cols = keep.tile([P, 8], F32, name="small_cols")
-        nc.vector.tensor_copy(small_cols[:], small_turned[:, 0:8])
+        small_cols = keep.tile([P, 2 * TILES], F32, name="small_cols")
+        nc.vector.tensor_copy(small_cols[:], small_turned[:, 0 : 2 * TILES])
         cap_wide = psum.tile([P, S], F32, name="cap_wide")
         for c in range(TILES):
             nc.tensor.transpose(
@@ -102,11 +107,11 @@ def tile_picked_yglovw_loss_p_kernel(
         for g in range(PASSES):
             nc.vector.tensor_copy(x_code[g][:], word_table[g][:].bitcast(U32).indirect(offsets[:]))
 
-
         powered = keep.tile([P, 2, 2, S], F32, name="powered")
         for b in range(2):
             nc.scalar.activation(powered[:, :, b, :], logc[:, :, b, :], ACT.Exp, bias=-POWER * SHIFT, scale=POWER)
-        flat = [r[:].rearrange("p j t -> p (j t)") for r in raw]
+
+        flat = [piece[:].rearrange("p j t -> p (j t)") for piece in raw]
         weight = [flat[b].rearrange("p (a s) -> p a s", a=2) for b in range(2)]
 
         def cap_weights(b):
@@ -114,12 +119,8 @@ def tile_picked_yglovw_loss_p_kernel(
                 weight[b], powered[:, :, b, :], cap_wide[:].unsqueeze(1).to_broadcast([P, 2, S]), ALU.min
             )
 
-        H = S // 2
-        spans = [[(0, S)]] * (TILES - 1) + [[(0, H), (H, S)]]
-        acc = [
-            [psum.tile([P, b - a], F32, name=f"acc{m}_{a}") for a, b in spans[m]] for m in range(TILES)
-        ]
-        sq = [flat[4], flat[3], flat[2][:, 0:S], flat[2][:, S : 2 * S]]
+        acc = [[psum.tile([P, hi - lo], F32, name=f"acc{m}_{lo}") for lo, hi in SPANS[m]] for m in range(TILES)]
+        square = [flat[4], flat[3], flat[2][:, 0:S], flat[2][:, S : 2 * S]]
         pair = keep.tile([P, 2 * S], F32, name="pair", align_bytes=64)
         err_tiles = [keep.tile([P, S], F32, name=f"err{m}") for m in (0, 1, 3)]
         err = [err_tiles[0][:], err_tiles[1][:], pair[:, 0:S], err_tiles[2][:]]
@@ -127,54 +128,57 @@ def tile_picked_yglovw_loss_p_kernel(
         res = [pair[:, S : 2 * S], res_tiles[0][:], diff[3][:], res_tiles[1][:]]
 
         def product(i):
-            c0, w, g, eng = pieces[i]
-            if i == 4:
+            first, width, g = PIECES[i]
+            if i == LAST:
                 woven = pair[:, S - P : S + P].bitcast(BF16)
-            elif i < 2:
-                woven = diff[2 + i][:].bitcast(BF16)
+            elif first == 0:
+                woven = diff[2 + g][:].bitcast(BF16)
             else:
-                woven_tile = keep.tile([P, w * PACK], BF16, name=f"woven{i}", align_bytes=64)
+                woven_tile = keep.tile([P, width * PACK], BF16, name=f"woven{i}", align_bytes=64)
                 woven = woven_tile[:]
-            dst = woven.rearrange("p (c i j) -> p c j i", i=4, j=PACK)
-            src = raw[i][:].rearrange("p j (c i) -> p c j i", i=4)
-            if eng == "v":
+            dst = woven.rearrange("p (c i j) -> p c j i", i=RUN, j=PACK)
+            src = raw[i][:].rearrange("p j (c i) -> p c j i", i=RUN)
+            if i == FIRST:
                 nc.vector.tensor_copy(dst, src)
             else:
                 nc.scalar.copy(dst, src)
-            h_code = keep.tile([P, w], U32, name=f"h_code{i}", align_bytes=64)
-            h_scale = keep.tile([P, w], U8, name=f"h_scale{i}", align_bytes=64)
+            h_code = keep.tile([P, width], U32, name=f"h_code{i}", align_bytes=64)
+            h_scale = keep.tile([P, width], U8, name=f"h_scale{i}", align_bytes=64)
             nc.vector.quantize_mx(out=h_code[:].bitcast(FP8X4), scales=h_scale[:], in_=woven)
-            for c in range(0, w, P):
-                m = (c0 + c) // P
-                for n, (a, b) in enumerate(spans[m]):
+            for c in range(0, width, P):
+                m = (first + c) // P
+                for n, (lo, hi) in enumerate(SPANS[m]):
                     nc.tensor.matmul_mx(
                         out=acc[m][n][:],
                         lhsT=h_code[:, c : c + P].bitcast(FP8X4),
                         lhsT_scale=h_scale[:, c : c + P],
-                        rhs=x_code[g][:, a:b].bitcast(FP8X4),
-                        rhs_scale=x_scale[4 * g : P, a:b],
+                        rhs=x_code[g][:, lo:hi].bitcast(FP8X4),
+                        rhs_scale=x_scale[SCALE_ROWS * g : P, lo:hi],
                         start=(g == 0),
                         stop=(g == PASSES - 1),
                     )
 
-        def error(m, n=0):
-            a, b = spans[m][n]
-            nc.vector.scalar_tensor_tensor(
-                err[m][:, a:b], acc[m][n][:], small_cols[:, 4 + m : 5 + m], diff[m][:, a:b], ALU.add, ALU.add
-            )
+        def error(m):
+            for n, (lo, hi) in enumerate(SPANS[m]):
+                nc.vector.scalar_tensor_tensor(
+                    err[m][:, lo:hi],
+                    acc[m][n][:],
+                    small_cols[:, TILES + m : TILES + m + 1],
+                    diff[m][:, lo:hi],
+                    ALU.add,
+                    ALU.add,
+                )
 
-        def finish(m, engine, n=0):
-            a, b = spans[m][n]
-            nc.scalar.activation(sq[m][:, a:b], err[m][:, a:b], ACT.Square)
-            engine.tensor_tensor(res[m][:, a:b], sq[m][:, a:b], weight[m % 2][:, m // 2, a:b], ALU.mult)
-            nc.sync.dma_start(out[m * P : (m + 1) * P, a:b], res[m][:, a:b])
+        def finish(m, engine):
+            for lo, hi in SPANS[m]:
+                nc.scalar.activation(square[m][:, lo:hi], err[m][:, lo:hi], ACT.Square)
+                engine.tensor_tensor(res[m][:, lo:hi], square[m][:, lo:hi], weight[m % 2][:, m // 2, lo:hi], ALU.mult)
+                nc.sync.dma_start(out[m * P : (m + 1) * P, lo:hi], res[m][:, lo:hi])
 
-        product(0)
-        cap_weights(0)
-        difference(2, nc.gpsimd)
-        product(1)
-        cap_weights(1)
-        difference(3, nc.gpsimd)
+        for b in range(2):
+            product(b)
+            cap_weights(b)
+            difference(2 + b, nc.gpsimd)
         product(2)
         error(0)
         product(3)
@@ -182,9 +186,6 @@ def tile_picked_yglovw_loss_p_kernel(
         error(1)
         finish(0, nc.gpsimd)
         error(2)
-        error(3, 0)
-        error(3, 1)
-        finish(1, nc.vector)
-        finish(2, nc.vector)
-        finish(3, nc.vector, 0)
-        finish(3, nc.vector, 1)
+        error(3)
+        for m in range(1, TILES):
+            finish(m, nc.vector)

from contextlib import ExitStack

import concourse.mybir as mybir
from concourse.masks import make_identity

K, T, S, V = 1024, 1024, 512, 512
FLOPS = 2 * K * V * S

F32 = mybir.dt.float32
BF16 = mybir.dt.bfloat16
I32 = mybir.dt.int32
U32 = mybir.dt.uint32
U16 = mybir.dt.uint16
U8 = mybir.dt.uint8
FP8X4 = mybir.dt.float8_e4m3fn_x4
ALU = mybir.AluOpType
ACT = mybir.ActivationFunctionType

P = 128
PACK = 4
PASSES = K // (P * PACK)
TILES = V // P
QUADRANTS = P // 32
SCALE_ROWS = 4
RUN = 4
POWER = 0.75
SHIFT = 2.3

PIECES = [(0, 2 * P, 0), (0, 2 * P, 1), (2 * P, 2 * P, 0), (2 * P, P, 1), (3 * P, P, 1)]
FIRST, LAST = 0, len(PIECES) - 1
SPANS = [[(0, S)]] * (TILES - 1) + [[(0, S // 2), (S // 2, S)]]


def tile_picked_yglovw_loss_p_kernel(
    tc, x_words, x_scales, hT, cooc, cap, ctxb, tgtb, offs, out
):
    nc = tc.nc
    with ExitStack() as stack:
        keep = stack.enter_context(tc.tile_pool(name="keep", bufs=1))
        psum = stack.enter_context(tc.psum_pool(name="psum", bufs=1))

        offsets = keep.tile([P, S // 16], U16, name="offsets")
        nc.sync.dma_start(offsets[:], offs)

        scale_table = keep.tile([P, T], U8, name="scale_table", align_bytes=64)
        nc.vector.memset(scale_table[:].bitcast(I32), 0)
        small_rows = keep.tile([P, P], F32, name="small_rows")
        nc.vector.memset(small_rows[:], 0.0)
        ident = keep.tile([P, P], F32, name="ident")
        make_identity(nc, ident[:])

        counts = [keep.tile([P, 2, S], F32, name=f"counts{a}") for a in range(2)]
        cooc_tiles = cooc.rearrange("(a b p) j -> a p b j", a=2, b=2)
        nc.sync.dma_start(counts[0][:], cooc_tiles[0])
        scales_i32 = x_scales.bitcast(I32)
        for q in range(QUADRANTS):
            nc.sync.dma_start(
                scale_table[32 * q : 32 * q + PASSES * SCALE_ROWS, :].bitcast(I32),
                scales_i32[:, SCALE_ROWS * q : SCALE_ROWS * (q + 1), :],
            )
        ctx_table = keep.tile([P, T], F32, name="ctx_table")
        nc.sync.dma_start(ctx_table[:], ctxb)
        nc.sync.dma_start(counts[1][:], cooc_tiles[1])

        word_table = [keep.tile([P, T], I32, name=f"word_table{g}") for g in range(PASSES)]
        words_i32 = [x_words[g].rearrange("p c r -> p (c r)").bitcast(I32) for g in range(PASSES)]
        nc.sync.dma_start(word_table[0][:], words_i32[0])
        nc.sync.dma_start(small_rows[0:TILES, :], cap[0:1, :].rearrange("o (c p) -> (o c) p", p=P))
        nc.sync.dma_start(small_rows[TILES : 2 * TILES, :], tgtb.rearrange("(c p) o -> c (p o)", p=P))
        nc.sync.dma_start(word_table[1][:], words_i32[1])

        h_passes = hT.rearrange("(g p j) t -> g p j t", g=PASSES, j=PACK)
        raw = []
        for i, (first, width, g) in enumerate(PIECES):
            piece = keep.tile([P, PACK, width], F32, name=f"raw{i}")
            nc.sync.dma_start(piece[:], h_passes[g][:, :, first : first + width])
            raw.append(piece)

        x_scale = keep.tile([P, S], U8, name="x_scale", align_bytes=64)
        nc.vector.tensor_copy(x_scale[:], scale_table[:].indirect(offsets[:]))
        ctx_picked = keep.tile([P, S], F32, name="ctx_picked")
        nc.vector.tensor_copy(ctx_picked[:], ctx_table[:].indirect(offsets[:]))

        small_turned = psum.tile([P, P], F32, name="small_turned")
        nc.tensor.transpose(small_turned[:], small_rows[:], ident[:])
        small_cols = keep.tile([P, 2 * TILES], F32, name="small_cols")
        nc.vector.tensor_copy(small_cols[:], small_turned[:, 0 : 2 * TILES])
        cap_wide = psum.tile([P, S], F32, name="cap_wide")
        for c in range(TILES):
            nc.tensor.transpose(
                cap_wide[:, c * P : (c + 1) * P], small_cols[:, c : c + 1].to_broadcast([P, P]), ident[:]
            )

        logc = keep.tile([P, 2, 2, S], F32, name="logc")
        for a in range(2):
            nc.scalar.activation(logc[:, a], counts[a][:], ACT.Ln)

        diff = [keep.tile([P, S], F32, name=f"diff{m}", align_bytes=64) for m in range(TILES)]

        def difference(m, engine):
            engine.tensor_tensor(diff[m][:], ctx_picked[:], logc[:, m // 2, m % 2, :], ALU.subtract)

        difference(0, nc.vector)
        difference(1, nc.vector)

        x_code = [keep.tile([P, S], U32, name=f"x_code{g}", align_bytes=64) for g in range(PASSES)]
        for g in range(PASSES):
            nc.vector.tensor_copy(x_code[g][:], word_table[g][:].bitcast(U32).indirect(offsets[:]))

        powered = keep.tile([P, 2, 2, S], F32, name="powered")
        for b in range(2):
            nc.scalar.activation(powered[:, :, b, :], logc[:, :, b, :], ACT.Exp, bias=-POWER * SHIFT, scale=POWER)

        flat = [piece[:].rearrange("p j t -> p (j t)") for piece in raw]
        weight = [flat[b].rearrange("p (a s) -> p a s", a=2) for b in range(2)]

        def cap_weights(b):
            nc.vector.tensor_tensor(
                weight[b], powered[:, :, b, :], cap_wide[:].unsqueeze(1).to_broadcast([P, 2, S]), ALU.min
            )

        acc = [[psum.tile([P, hi - lo], F32, name=f"acc{m}_{lo}") for lo, hi in SPANS[m]] for m in range(TILES)]
        square = [flat[4], flat[3], flat[2][:, 0:S], flat[2][:, S : 2 * S]]
        pair = keep.tile([P, 2 * S], F32, name="pair", align_bytes=64)
        err_tiles = [keep.tile([P, S], F32, name=f"err{m}") for m in (0, 1, 3)]
        err = [err_tiles[0][:], err_tiles[1][:], pair[:, 0:S], err_tiles[2][:]]
        res_tiles = [keep.tile([P, S], F32, name=f"res{m}") for m in (1, 3)]
        res = [pair[:, S : 2 * S], res_tiles[0][:], diff[3][:], res_tiles[1][:]]

        def product(i):
            first, width, g = PIECES[i]
            if i == LAST:
                woven = pair[:, S - P : S + P].bitcast(BF16)
            elif first == 0:
                woven = diff[2 + g][:].bitcast(BF16)
            else:
                woven_tile = keep.tile([P, width * PACK], BF16, name=f"woven{i}", align_bytes=64)
                woven = woven_tile[:]
            dst = woven.rearrange("p (c i j) -> p c j i", i=RUN, j=PACK)
            src = raw[i][:].rearrange("p j (c i) -> p c j i", i=RUN)
            if i == FIRST:
                nc.vector.tensor_copy(dst, src)
            else:
                nc.scalar.copy(dst, src)
            h_code = keep.tile([P, width], U32, name=f"h_code{i}", align_bytes=64)
            h_scale = keep.tile([P, width], U8, name=f"h_scale{i}", align_bytes=64)
            nc.vector.quantize_mx(out=h_code[:].bitcast(FP8X4), scales=h_scale[:], in_=woven)
            for c in range(0, width, P):
                m = (first + c) // P
                for n, (lo, hi) in enumerate(SPANS[m]):
                    nc.tensor.matmul_mx(
                        out=acc[m][n][:],
                        lhsT=h_code[:, c : c + P].bitcast(FP8X4),
                        lhsT_scale=h_scale[:, c : c + P],
                        rhs=x_code[g][:, lo:hi].bitcast(FP8X4),
                        rhs_scale=x_scale[SCALE_ROWS * g : P, lo:hi],
                        start=(g == 0),
                        stop=(g == PASSES - 1),
                    )

        def error(m):
            for n, (lo, hi) in enumerate(SPANS[m]):
                nc.vector.scalar_tensor_tensor(
                    err[m][:, lo:hi],
                    acc[m][n][:],
                    small_cols[:, TILES + m : TILES + m + 1],
                    diff[m][:, lo:hi],
                    ALU.add,
                    ALU.add,
                )

        def finish(m, engine):
            for lo, hi in SPANS[m]:
                nc.scalar.activation(square[m][:, lo:hi], err[m][:, lo:hi], ACT.Square)
                engine.tensor_tensor(res[m][:, lo:hi], square[m][:, lo:hi], weight[m % 2][:, m // 2, lo:hi], ALU.mult)
                nc.sync.dma_start(out[m * P : (m + 1) * P, lo:hi], res[m][:, lo:hi])

        for b in range(2):
            product(b)
            cap_weights(b)
            difference(2 + b, nc.gpsimd)
        product(2)
        error(0)
        product(3)
        product(4)
        error(1)
        finish(0, nc.gpsimd)
        error(2)
        error(3)
        for m in range(1, TILES):
            finish(m, nc.vector)
